import numpy as np
import ml_dtypes


def mxq(x, axis, fmt="e4m3"):
    dtype, down = {"e4m3": (ml_dtypes.float8_e4m3fn, 7), "e5m2": (ml_dtypes.float8_e5m2, 14)}[fmt]
    v = np.moveaxis(np.asarray(x, np.float32).astype(ml_dtypes.bfloat16).astype(np.float64), axis, -1)
    blocks = v.reshape(v.shape[:-1] + (-1, 32))
    amax = np.abs(blocks).max(-1, keepdims=True)
    byte = np.maximum(np.where(amax > 0, np.frexp(amax)[1] - 1 + 127, 0) - down, 1)
    scale = np.exp2(byte - 127.0)
    codes = (blocks / scale).astype(np.float32).astype(dtype).astype(np.float64)
    return np.moveaxis((codes * scale).reshape(v.shape), -1, axis)


WIDE = False


def mx_kscale(k):
    if not WIDE:
        return np.ones(k)
    levels = np.array([10, -10, 5, -5, 0])
    if k % 512:
        return np.exp2(np.random.permutation(np.resize(levels, k // 32))).repeat(32)
    a = np.empty((k // 512, 16))
    for p in range(k // 512):
        a[p, :8] = np.random.permutation(np.resize(levels, 8))
        for g in range(8):
            far = levels[np.abs(levels - a[p, g]) >= 10]
            a[p, g + 8] = far[np.random.randint(len(far))]
    return np.exp2(a.ravel()).repeat(32)


def f64(x):
    return np.asarray(x).astype(np.float64)


def striped(idx):
    return np.tile(np.asarray(idx).reshape(-1, 16).T, (8, 1)).astype(np.uint16)


def unstriped(offs):
    return offs[:16].T.reshape(-1).astype(np.int64)


E2M1 = np.array([0.0, 0.5, 1.0, 1.5, 2.0, 3.0, 4.0, 6.0, -0.0, -0.5, -1.0, -1.5, -2.0, -3.0, -4.0, -6.0])


def pack_weight(w, fmt):
    k, n = w.shape
    w = f64(np.asarray(w, np.float32).astype(ml_dtypes.bfloat16)).reshape(k // 32, 32, n)
    amax = np.abs(w).max(1)
    if fmt == "e4m3":
        byte = np.frexp(amax)[1] - 1 + 127 - 7
    else:
        mant, ex = np.frexp(amax / 6.0)
        byte = np.where(mant > 0.5, ex, ex - 1) + 127
    byte = np.clip(np.where(amax > 0, byte, 1), 1, 254)
    scaled = (w * np.exp2(127.0 - byte)[:, None, :]).reshape(k, n).astype(np.float32)
    by_word = np.ascontiguousarray(scaled.reshape(k // 512, 128, 4, n).transpose(0, 1, 3, 2))
    if fmt == "e4m3":
        words = by_word.astype(ml_dtypes.float8_e4m3fn).view(np.uint8)
    else:
        c = by_word.astype(ml_dtypes.float4_e2m1fn).view(np.uint8) & 0xF
        words = (c[..., 0::2] | (c[..., 1::2] << 4)).reshape(k // 512, 128, 2 * n)
    return np.ascontiguousarray(words), np.ascontiguousarray(byte.astype(np.uint8).reshape(k // 512, 16, n))


def unpack_weight(words, scales, fmt):
    g, _, n = scales.shape
    words = np.ascontiguousarray(words).reshape(g, 128, n, -1)
    if fmt == "e4m3":
        vals = words.view(ml_dtypes.float8_e4m3fn).astype(np.float64)
    else:
        nib = np.empty((g, 128, n, 4), np.uint8)
        nib[..., 0::2] = words & 0xF
        nib[..., 1::2] = words >> 4
        vals = E2M1[nib]
    vals = vals * np.repeat(np.exp2(scales.astype(np.float64) - 127.0), 8, axis=1)[..., None]
    return vals.transpose(0, 1, 3, 2).reshape(g * 512, n)


def sigmoid(v):
    return 1.0 / (1.0 + np.exp(-v))


def sgn(shape):
    return np.random.uniform(0.5, 2.0, shape) * np.where(np.random.standard_normal(shape) < 0, -1.0, 1.0)


K, T, J, R, F, Z, O, N, L, E = 512, 1024, 256, 512, 512, 1024, 128, 256, 512, 512


def setup_inputs():
    n = np.random.standard_normal
    idx = np.random.permutation(T)[:J]
    idx2 = np.random.permutation(Z)[:J]
    idx3 = np.random.permutation(J)[:O]
    idx4 = np.random.permutation(J)[:O]
    idx5 = np.random.permutation(J)[:O]
    idx6 = np.random.permutation(E)[:O]
    idx7 = np.random.permutation(E)[:O]
    ff = mx_kscale(F)
    fk = mx_kscale(K)
    fr = mx_kscale(R)
    fl = mx_kscale(L)
    xop = pack_weight(n((F, Z)) / ff[:, None], "e4m3")
    wp = pack_weight(n((K, R)) * 1 / np.sqrt(K) / fk[:, None], "e2m1")
    w2p = pack_weight(n((F, R)) * 1 / np.sqrt(F) * ff[:, None], "e2m1")
    wbp = pack_weight(n((R, N)) * 1 / np.sqrt(R) / fr[:, None], "e2m1")
    sxp = pack_weight(n((L, O)) / fl[:, None], "e4m3")
    wsp = pack_weight(n((L, N)) * 1 / np.sqrt(L) * fl[:, None], "e2m1")
    return {
        "xo_words": xop[0],
        "xo_scales": xop[1],
        "cq": (np.random.randint(-7, 8, (K, T)).astype(np.float64)).astype(np.float32),
        "gs": (np.random.uniform(0.1, 0.4, (K, 1)) * fk[:, None]).astype(np.float32),
        "w_words": wp[0],
        "w_scales": wp[1],
        "w2_words": w2p[0],
        "w2_scales": w2p[1],
        "sa": (np.random.uniform(0.5, 1.6, (R, 1)) * fr[:, None]).astype(np.float32),
        "sb": (np.random.uniform(0.5, 1.6, (R, 1)) * fr[:, None]).astype(np.float32),
        "sg": (sgn((R, 1))).astype(np.float32),
        "bg": (np.random.uniform(-2.0, 2.0, (R, 1))).astype(np.float32),
        "wb_words": wbp[0],
        "wb_scales": wbp[1],
        "sx_words": sxp[0],
        "sx_scales": sxp[1],
        "ws_words": wsp[0],
        "ws_scales": wsp[1],
        "offs": striped(idx),
        "offs2": striped(idx2),
        "offs3": striped(idx3),
        "offs4": striped(idx4),
        "offs5": striped(idx5),
        "offs6": striped(idx6),
        "offs7": striped(idx7),
    }


def reference(xo_words, xo_scales, cq, gs, w_words, w_scales, w2_words, w2_scales, sa, sb, sg, bg, wb_words, wb_scales, sx_words, sx_scales, ws_words, ws_scales, offs, offs2, offs3, offs4, offs5, offs6, offs7):
    idx = unstriped(offs)
    idx2 = unstriped(offs2)
    idx3 = unstriped(offs3)
    idx4 = unstriped(offs4)
    idx5 = unstriped(offs5)
    idx6 = unstriped(offs6)
    idx7 = unstriped(offs7)
    xou = unpack_weight(xo_words, xo_scales, "e4m3")
    wu = unpack_weight(w_words, w_scales, "e2m1")
    w2u = unpack_weight(w2_words, w2_scales, "e2m1")
    wbu = unpack_weight(wb_words, wb_scales, "e2m1")
    sxu = unpack_weight(sx_words, sx_scales, "e4m3")
    wsu = unpack_weight(ws_words, ws_scales, "e2m1")
    x1 = f64(cq)[:, idx] * f64(gs)
    x1q = mxq(x1, 0, "e4m3")
    a = wu.T @ x1q
    xoidx2g = xou[:, idx2]
    b = w2u.T @ xoidx2g
    hid = np.minimum(a[:, idx3] * f64(sa) * sigmoid(b[:, idx4] * f64(sg) + f64(bg)), b[:, idx5] * f64(sb))
    hidq = mxq(hid, 0, "e4m3")
    p = wbu.T @ hidq + wsu.T @ sxu
    pa = np.zeros((N, E))
    pa[:, idx6] = p
    pb = np.zeros((N, E))
    pb[:, idx7] = p
    y = pa + pb
    return y

@@ -1,0 +1,243 @@
+from contextlib import ExitStack
+
+import concourse.mybir as mybir
+
+K, T, J, R, F, Z, O, N, L, E = 512, 1024, 256, 512, 512, 1024, 128, 256, 512, 512
+
+FLOPS = 2 * (K * R * J + F * R * J + R * N * O + L * N * O)
+
+F32 = mybir.dt.float32
+BF16 = mybir.dt.bfloat16
+I32 = mybir.dt.int32
+U32 = mybir.dt.uint32
+U16 = mybir.dt.uint16
+U8 = mybir.dt.uint8
+FP8X4 = mybir.dt.float8_e4m3fn_x4
+FP4X4 = mybir.dt.float4_e2m1fn_x4
+ACT = mybir.ActivationFunctionType
+ALU = mybir.AluOpType
+
+P = 128
+PACK = 4
+QUAD = 32
+LIVE = 4
+
+
+def tile_list_gatedmiddle_codednote_further_pagetwice_kernel(
+    tc, xo_words, xo_scales, cq, gs, w_words, w_scales, w2_words, w2_scales, sa, sb, sg, bg,
+    wb_words, wb_scales, sx_words, sx_scales, ws_words, ws_scales,
+    offs, offs2, offs3, offs4, offs5, offs6, offs7, out,
+):
+    nc = tc.nc
+    with ExitStack() as ctx:
+        lists = ctx.enter_context(tc.tile_pool(name="lists", bufs=1))
+        keep = ctx.enter_context(tc.tile_pool(name="keep", bufs=1))
+        psum = ctx.enter_context(tc.psum_pool(name="psum", bufs=1))
+
+        def load_list(src, name):
+            held = lists.tile(list(src.shape), U16, name=name)
+            nc.sync.dma_start(held[:], src)
+            return held
+
+        def load_words(src, name):
+            rows = src[0] if src.ndim == 3 else src[0].rearrange("p n t -> p (n t)")
+            held = keep.tile([P, rows.shape[1]], U8, name=name, align_bytes=64)
+            nc.sync.dma_start(held[:].bitcast(I32), rows.bitcast(I32))
+            return held
+
+        def load_column(src, name, queue):
+            held = keep.tile([P, PACK], F32, name=name)
+            queue.dma_start(held[:], src.rearrange("(p t) o -> p (t o)", t=PACK))
+            return held
+
+        def stage_scales(staged, src, column, queue):
+            words = src.shape[2] // 4
+            queue.dma_start(
+                staged[:, :, column : column + words], src[0].bitcast(I32).rearrange("(q r) n -> r q n", r=LIVE)
+            )
+
+        def deal_words(words, name, copy):
+            dealt = keep.tile([P, 2 * R], U8, name=name, align_bytes=64)
+            copy(
+                dealt[:].bitcast(U16).rearrange("p (t m) -> p t m", t=PACK),
+                words[:].bitcast(U16).rearrange("p (m t) -> p t m", t=PACK),
+            )
+            return dealt
+
+        def deal_scales(plane, name):
+            dealt = keep.tile([P, R], U8, name=name, align_bytes=64)
+            nc.vector.tensor_copy(
+                dealt[:].rearrange("p (t m) -> p t m", t=PACK),
+                plane.bitcast(U8).rearrange("p (m t) -> p t m", t=PACK),
+            )
+            return dealt
+
+        def load_cq(t):
+            rows = keep.tile([P, T], F32, name="cq%d" % t, tag="cq%d" % t)
+            nc.sync.dma_start(rows[:], cq.rearrange("(p t) c -> p t c", t=PACK)[:, t, :])
+            return rows
+
+        idx2 = load_list(offs2, "idx2")
+        xo_staged = keep.tile([LIVE, 4, Z // 4], I32)
+        stage_scales(xo_staged[:], xo_scales, 0, nc.scalar)
+        xo_raw = load_words(xo_words, "xo_raw")
+        first_staged = keep.tile([P, 4, 2 * R // 4], I32)
+        nc.vector.memset(first_staged[64:96], 0)
+        stage_scales(first_staged[64 : 64 + LIVE], w2_scales, 0, nc.scalar)
+        stage_scales(first_staged[64 : 64 + LIVE], w_scales, R // 4, nc.scalar)
+        idx = load_list(offs, "idx")
+        w2_raw = load_words(w2_words, "w2_raw")
+        gs_col = load_column(gs, "gs_col", nc.gpsimd)
+        sg_col = load_column(sg, "sg_col", nc.gpsimd)
+        bg_col = load_column(bg, "bg_col", nc.gpsimd)
+        sb_col = load_column(sb, "sb_col", nc.gpsimd)
+        cq_rows = [load_cq(0), load_cq(1)]
+        last_staged = keep.tile([P, 4, (2 * N + O) // 4], I32, align_bytes=64)
+        nc.vector.memset(last_staged[:, 0, :], 0)
+        stage_scales(last_staged[0:LIVE], ws_scales, 0, nc.sync)
+        stage_scales(last_staged[0:LIVE], wb_scales, N // 4, nc.sync)
+        stage_scales(last_staged[0:LIVE], sx_scales, 2 * N // 4, nc.sync)
+        cq_rows.append(load_cq(2))
+        idx4 = load_list(offs4, "idx4")
+        cq_rows.append(load_cq(3))
+        w_raw = load_words(w_words, "w_raw")
+        idx5 = load_list(offs5, "idx5")
+        idx3 = load_list(offs3, "idx3")
+        sa_col = load_column(sa, "sa_col", nc.sync)
+        ws_raw = load_words(ws_words, "ws_raw")
+        sx_raw = load_words(sx_words, "sx_raw")
+        wb_raw = load_words(wb_words, "wb_raw")
+        idx6 = load_list(offs6, "idx6")
+        idx7 = load_list(offs7, "idx7")
+
+        xo_plane = keep.tile([P, Z], U8)
+        nc.vector.memset(xo_plane[:].bitcast(I32), 0)
+        for q in range(4):
+            nc.vector.tensor_copy(xo_plane[QUAD * q : QUAD * q + LIVE, :].bitcast(I32), xo_staged[:, q, :])
+        xg_scales = keep.tile([P, J], U8, align_bytes=64)
+        nc.vector.tensor_copy(xg_scales[:], xo_plane[:].indirect(idx2[:]))
+        xg_words = keep.tile([P, J], U32, align_bytes=64)
+        nc.vector.tensor_copy(xg_words[:], xo_raw[:].bitcast(U32).indirect(idx2[:]))
+        for q in (0, 1, 3):
+            nc.vector.tensor_copy(first_staged[QUAD * q : QUAD * (q + 1), 2, :], first_staged[64:96, q, :])
+        w2_plane = deal_scales(first_staged[:, 2, 0 : R // 4], "w2_plane")
+        w2_dealt = deal_words(w2_raw, "w2_dealt", nc.scalar.copy)
+
+        def first_stage(words, plane, rhs_words, rhs_scales, name):
+            tiles = []
+            for t in range(PACK):
+                acc = psum.tile([P, J], F32, name="acc%d" % t)
+                nc.tensor.matmul_mx(
+                    out=acc[:],
+                    lhsT=words[:, 2 * P * t : 2 * P * (t + 1)].bitcast(FP4X4),
+                    lhsT_scale=plane[:, P * t : P * (t + 1)],
+                    rhs=rhs_words[:].bitcast(FP8X4),
+                    rhs_scale=rhs_scales[:],
+                    start=True,
+                    stop=True,
+                )
+                rows = keep.tile([P, J], F32, name="%s%d" % (name, t))
+                nc.vector.tensor_copy(rows[:], acc[:])
+                tiles.append(rows)
+            return tiles
+
+        b_rows = first_stage(w2_dealt, w2_plane, xg_words, xg_scales, "b")
+        w_plane = deal_scales(first_staged[:, 2, R // 4 : 2 * R // 4], "w_plane")
+
+        x1_rows = keep.tile([P, PACK, J], BF16)
+        for t in range(PACK):
+            nc.scalar.activation(
+                x1_rows[:, t, :], cq_rows[t][:].indirect(idx[:]), ACT.Copy, scale=gs_col[:, t : t + 1]
+            )
+        gate_first = keep.tile([P, O], F32)
+        gate_rest = keep.tile([P, PACK - 1, O], F32, tag="cq%d" % (PACK - 1))
+        gate = [gate_first[:]] + [gate_rest[:, t, :] for t in range(PACK - 1)]
+        for t in range(PACK):
+            nc.scalar.activation(
+                gate[t], b_rows[t][:].indirect(idx4[:]), ACT.Sigmoid,
+                bias=bg_col[:, t : t + 1], scale=sg_col[:, t : t + 1],
+            )
+        x1_grouped = keep.tile([P, J * PACK], BF16, align_bytes=64)
+        nc.vector.tensor_copy(
+            x1_grouped[:].rearrange("p (c i t) -> p c t i", i=4, t=PACK),
+            x1_rows[:].rearrange("p t (c i) -> p c t i", i=4),
+        )
+        w_dealt = deal_words(w_raw, "w_dealt", nc.vector.tensor_copy)
+        x1_words = keep.tile([P, J], U32, align_bytes=64)
+        x1_scales = keep.tile([P, J], U8, align_bytes=64)
+        nc.vector.quantize_mx(out=x1_words[:].bitcast(FP8X4), scales=x1_scales[:], in_=x1_grouped[:])
+        a_rows = first_stage(w_dealt, w_plane, x1_words, x1_scales, "a")
+
+        for q in (1, 2, 3):
+            nc.vector.tensor_copy(last_staged[QUAD * q : QUAD * q + LIVE, 0, :], last_staged[0:LIVE, q, :])
+        last_planes = last_staged[:, 0, :].bitcast(U8)
+        ws_plane = last_planes[:, 0:N]
+        wb_plane = last_planes[:, N : 2 * N]
+        sx_plane = last_planes[:, 2 * N : 2 * N + O]
+        halves = range(N // P)
+        p_acc = [psum.tile([P, O], F32, name="p_acc%d" % h) for h in halves]
+        for h in halves:
+            nc.tensor.matmul_mx(
+                out=p_acc[h][:],
+                lhsT=ws_raw[:, 2 * P * h : 2 * P * (h + 1)].bitcast(FP4X4),
+                lhsT_scale=ws_plane[:, P * h : P * (h + 1)],
+                rhs=sx_raw[:].bitcast(FP8X4),
+                rhs_scale=sx_plane,
+                start=True,
+                stop=False,
+            )
+        page_a = [keep.tile([P, E], F32, name="page_a%d" % h) for h in halves]
+        page_b = [keep.tile([P, E], F32, name="page_b%d" % h) for h in halves]
+        for page in page_a + page_b:
+            nc.vector.memset(page[:], 0.0)
+
+        a_term = keep.tile([P, PACK, O], F32)
+        gated = keep.tile([P, PACK, O], F32)
+        for t in range(PACK):
+            nc.scalar.activation(
+                a_term[:, t, :], a_rows[t][:].indirect(idx3[:]), ACT.Copy, scale=sa_col[:, t : t + 1]
+            )
+            nc.vector.tensor_tensor(gated[:, t, :], a_term[:, t, :], gate[t], ALU.mult)
+        b_term = keep.tile([P, PACK, O], F32)
+        for t in range(PACK):
+            nc.scalar.activation(
+                b_term[:, t, :], b_rows[t][:].indirect(idx5[:]), ACT.Copy, scale=sb_col[:, t : t + 1]
+            )
+        hid_grouped = keep.tile([P, O * PACK], BF16, align_bytes=64)
+        nc.vector.tensor_tensor(
+            hid_grouped[:].rearrange("p (c i t) -> p c t i", i=4, t=PACK),
+            gated[:].rearrange("p t (c i) -> p c t i", i=4),
+            b_term[:].rearrange("p t (c i) -> p c t i", i=4),
+            ALU.min,
+        )
+        hid_words = keep.tile([P, O], U32, align_bytes=64)
+        hid_scales = keep.tile([P, O], U8, align_bytes=64)
+        nc.vector.quantize_mx(out=hid_words[:].bitcast(FP8X4), scales=hid_scales[:], in_=hid_grouped[:])
+
+        p_rows = []
+        for h in halves:
+            nc.tensor.matmul_mx(
+                out=p_acc[h][:],
+                lhsT=wb_raw[:, 2 * P * h : 2 * P * (h + 1)].bitcast(FP4X4),
+                lhsT_scale=wb_plane[:, P * h : P * (h + 1)],
+                rhs=hid_words[:].bitcast(FP8X4),
+                rhs_scale=hid_scales[:],
+                start=False,
+                stop=True,
+            )
+            rows = keep.tile([P, O], F32, name="p_rows%d" % h)
+            if h == 0:
+                nc.vector.tensor_copy(rows[:], p_acc[h][:])
+            else:
+                nc.scalar.copy(rows[:], p_acc[h][:])
+            p_rows.append(rows)
+        for h in halves:
+            nc.scalar.activation(page_a[h][:].indirect(idx6[:]), p_rows[h][:], ACT.Copy)
+            nc.vector.tensor_copy(page_b[h][:].indirect(idx7[:]), p_rows[h][:])
+        for h in halves:
+            for c in range(2):
+                cols = slice(c * E // 2, (c + 1) * E // 2)
+                total = keep.tile([P, E // 2], F32, name="total%d%d" % (h, c))
+                nc.vector.tensor_tensor(total[:], page_a[h][:, cols], page_b[h][:, cols], ALU.add)
+                queue = nc.sync if c == 0 else nc.scalar
+                queue.dma_start(out[P * h : P * (h + 1), cols], total[:])

@@ -85,6 +85,10 @@ def tile_list_gatedmiddle_codednote_further_pagetwice_kernel(
         nc.vector.memset(first_staged[64:96], 0)
         stage_scales(first_staged[64 : 64 + LIVE], w2_scales, 0, nc.scalar)
         stage_scales(first_staged[64 : 64 + LIVE], w_scales, R // 4, nc.scalar)
+        warm_in = keep.tile([P, 1], F32)
+        warm_out = keep.tile([P, 1], F32)
+        nc.vector.memset(warm_in[:], 0.0)
+        nc.scalar.activation(warm_out[:], warm_in[:], ACT.Sigmoid)
         idx = load_list(offs, "idx")
         w2_raw = load_words(w2_words, "w2_raw")
         gs_col = load_column(gs, "gs_col", nc.gpsimd)

@@ -73,39 +73,40 @@ def tile_list_gatedmiddle_codednote_further_pagetwice_kernel(
             return dealt
 
         def load_cq(t):
-            rows = keep.tile([P, T], F32, name="cq%d" % t, tag="cq%d" % t)
+            rows = keep.tile([P, T], F32, name="cq%d" % t)
             nc.sync.dma_start(rows[:], cq.rearrange("(p t) c -> p t c", t=PACK)[:, t, :])
             return rows
 
+        xo_scale_rows = xo_scales[0].bitcast(I32).rearrange("(u q r) n -> u r q n", u=2, r=LIVE)
+        xo_staged = keep.tile([P, 2, Z // 4], I32)
+        nc.scalar.dma_start(xo_staged[0:LIVE], xo_scale_rows[0])
+        nc.sync.dma_start(xo_staged[64 : 64 + LIVE], xo_scale_rows[1])
         idx2 = load_list(offs2, "idx2")
-        xo_staged = keep.tile([LIVE, 4, Z // 4], I32)
-        stage_scales(xo_staged[:], xo_scales, 0, nc.scalar)
+        first_staged = keep.tile([LIVE, 4, 2 * R // 4], I32)
+        stage_scales(first_staged[:], w2_scales, 0, nc.scalar)
+        stage_scales(first_staged[:], w_scales, R // 4, nc.scalar)
         xo_raw = load_words(xo_words, "xo_raw")
-        first_staged = keep.tile([P, 4, 2 * R // 4], I32)
-        nc.vector.memset(first_staged[64:96], 0)
-        stage_scales(first_staged[64 : 64 + LIVE], w2_scales, 0, nc.scalar)
-        stage_scales(first_staged[64 : 64 + LIVE], w_scales, R // 4, nc.scalar)
-        warm_in = keep.tile([P, 1], F32)
-        warm_out = keep.tile([P, 1], F32)
-        nc.vector.memset(warm_in[:], 0.0)
-        nc.scalar.activation(warm_out[:], warm_in[:], ACT.Sigmoid)
-        idx = load_list(offs, "idx")
         w2_raw = load_words(w2_words, "w2_raw")
-        gs_col = load_column(gs, "gs_col", nc.gpsimd)
-        sg_col = load_column(sg, "sg_col", nc.gpsimd)
-        bg_col = load_column(bg, "bg_col", nc.gpsimd)
-        sb_col = load_column(sb, "sb_col", nc.gpsimd)
-        cq_rows = [load_cq(0), load_cq(1)]
+        cq_rows = [load_cq(0)]
+        idx = load_list(offs, "idx")
+        gs_col = load_column(gs, "gs_col", nc.sync)
+        cq_rows.extend([load_cq(1), load_cq(2)])
+        w_raw = load_words(w_words, "w_raw")
+        xo_plane = keep.tile([P, Z], U8)
+        nc.vector.memset(xo_plane[:].bitcast(I32), 0)
+        first_spread = keep.tile([P, 2 * R // 4], I32)
+        nc.vector.memset(first_spread[:], 0)
         last_staged = keep.tile([P, 4, (2 * N + O) // 4], I32, align_bytes=64)
         nc.vector.memset(last_staged[:, 0, :], 0)
         stage_scales(last_staged[0:LIVE], ws_scales, 0, nc.sync)
+        cq_rows.append(load_cq(3))
         stage_scales(last_staged[0:LIVE], wb_scales, N // 4, nc.sync)
         stage_scales(last_staged[0:LIVE], sx_scales, 2 * N // 4, nc.sync)
-        cq_rows.append(load_cq(2))
+        sg_col = load_column(sg, "sg_col", nc.sync)
+        bg_col = load_column(bg, "bg_col", nc.sync)
         idx4 = load_list(offs4, "idx4")
-        cq_rows.append(load_cq(3))
-        w_raw = load_words(w_words, "w_raw")
         idx5 = load_list(offs5, "idx5")
+        sb_col = load_column(sb, "sb_col", nc.sync)
         idx3 = load_list(offs3, "idx3")
         sa_col = load_column(sa, "sa_col", nc.sync)
         ws_raw = load_words(ws_words, "ws_raw")
@@ -114,17 +115,28 @@ def tile_list_gatedmiddle_codednote_further_pagetwice_kernel(
         idx6 = load_list(offs6, "idx6")
         idx7 = load_list(offs7, "idx7")
 
-        xo_plane = keep.tile([P, Z], U8)
-        nc.vector.memset(xo_plane[:].bitcast(I32), 0)
+        halves = range(N // P)
+        page_a = [keep.tile([P, E], F32, name="page_a%d" % h) for h in halves]
+        page_b = [keep.tile([P, E], F32, name="page_b%d" % h) for h in halves]
+        for page in page_a + page_b:
+            nc.vector.memset(page[:], 0.0)
+        warm_in = keep.tile([P, 1], F32)
+        warm_out = keep.tile([P, 1], F32)
+        nc.vector.memset(warm_in[:], 0.0)
+        nc.scalar.activation(warm_out[:], warm_in[:], ACT.Sigmoid)
+
         for q in range(4):
-            nc.vector.tensor_copy(xo_plane[QUAD * q : QUAD * q + LIVE, :].bitcast(I32), xo_staged[:, q, :])
+            first = 64 * (q // 2)
+            nc.vector.tensor_copy(
+                xo_plane[QUAD * q : QUAD * q + LIVE, :].bitcast(I32), xo_staged[first : first + LIVE, q % 2, :]
+            )
         xg_scales = keep.tile([P, J], U8, align_bytes=64)
         nc.vector.tensor_copy(xg_scales[:], xo_plane[:].indirect(idx2[:]))
         xg_words = keep.tile([P, J], U32, align_bytes=64)
         nc.vector.tensor_copy(xg_words[:], xo_raw[:].bitcast(U32).indirect(idx2[:]))
-        for q in (0, 1, 3):
-            nc.vector.tensor_copy(first_staged[QUAD * q : QUAD * (q + 1), 2, :], first_staged[64:96, q, :])
-        w2_plane = deal_scales(first_staged[:, 2, 0 : R // 4], "w2_plane")
+        for q in range(4):
+            nc.vector.tensor_copy(first_spread[QUAD * q : QUAD * q + LIVE, :], first_staged[:, q, :])
+        w2_plane = deal_scales(first_spread[:, 0 : R // 4], "w2_plane")
         w2_dealt = deal_words(w2_raw, "w2_dealt", nc.scalar.copy)
 
         def first_stage(words, plane, rhs_words, rhs_scales, name):
@@ -146,39 +158,47 @@ def tile_list_gatedmiddle_codednote_further_pagetwice_kernel(
             return tiles
 
         b_rows = first_stage(w2_dealt, w2_plane, xg_words, xg_scales, "b")
-        w_plane = deal_scales(first_staged[:, 2, R // 4 : 2 * R // 4], "w_plane")
+        w_plane = deal_scales(first_spread[:, R // 4 : 2 * R // 4], "w_plane")
 
-        x1_rows = keep.tile([P, PACK, J], BF16)
+        w_dealt = deal_words(w_raw, "w_dealt", nc.vector.tensor_copy)
+
+        x1_early = keep.tile([P, PACK - 1, J], BF16)
+        x1_last = keep.tile([P, J], BF16)
+        x1_rows = [x1_early[:, t, :] for t in range(PACK - 1)] + [x1_last[:]]
         for t in range(PACK):
-            nc.scalar.activation(
-                x1_rows[:, t, :], cq_rows[t][:].indirect(idx[:]), ACT.Copy, scale=gs_col[:, t : t + 1]
-            )
-        gate_first = keep.tile([P, O], F32)
-        gate_rest = keep.tile([P, PACK - 1, O], F32, tag="cq%d" % (PACK - 1))
-        gate = [gate_first[:]] + [gate_rest[:, t, :] for t in range(PACK - 1)]
+            nc.scalar.activation(x1_rows[t], cq_rows[t][:].indirect(idx[:]), ACT.Copy, scale=gs_col[:, t : t + 1])
+        b_term = keep.tile([P, PACK, O], F32)
+        gate_tile = keep.tile([P, PACK - 1, O], F32)
+        gate = [gate_tile[:, 0, :], gate_tile[:, 1, :], b_term[:, PACK - 1, :], gate_tile[:, 2, :]]
         for t in range(PACK):
             nc.scalar.activation(
                 gate[t], b_rows[t][:].indirect(idx4[:]), ACT.Sigmoid,
                 bias=bg_col[:, t : t + 1], scale=sg_col[:, t : t + 1],
             )
-        x1_grouped = keep.tile([P, J * PACK], BF16, align_bytes=64)
+        x1_grouped = keep.tile([P, J, PACK], BF16, align_bytes=64)
         nc.vector.tensor_copy(
-            x1_grouped[:].rearrange("p (c i t) -> p c t i", i=4, t=PACK),
-            x1_rows[:].rearrange("p t (c i) -> p c t i", i=4),
+            x1_grouped[:, :, 0 : PACK - 1].rearrange("p (c i) t -> p c t i", i=4),
+            x1_early[:].rearrange("p t (c i) -> p c t i", i=4),
         )
-        w_dealt = deal_words(w_raw, "w_dealt", nc.vector.tensor_copy)
         x1_words = keep.tile([P, J], U32, align_bytes=64)
         x1_scales = keep.tile([P, J], U8, align_bytes=64)
-        nc.vector.quantize_mx(out=x1_words[:].bitcast(FP8X4), scales=x1_scales[:], in_=x1_grouped[:])
-        a_rows = first_stage(w_dealt, w_plane, x1_words, x1_scales, "a")
-
+        slots = [slice(0, J // 2), slice(J // 2, J)]
+        for cols in slots:
+            nc.vector.tensor_copy(x1_grouped[:, cols, PACK - 1], x1_last[:, cols])
+        for cols in slots:
+            nc.vector.quantize_mx(
+                out=x1_words[:, cols].bitcast(FP8X4),
+                scales=x1_scales[:, cols],
+                in_=x1_grouped[:, cols, :].rearrange("p j t -> p (j t)"),
+            )
         for q in (1, 2, 3):
             nc.vector.tensor_copy(last_staged[QUAD * q : QUAD * q + LIVE, 0, :], last_staged[0:LIVE, q, :])
+        a_rows = first_stage(w_dealt, w_plane, x1_words, x1_scales, "a")
+
         last_planes = last_staged[:, 0, :].bitcast(U8)
         ws_plane = last_planes[:, 0:N]
         wb_plane = last_planes[:, N : 2 * N]
         sx_plane = last_planes[:, 2 * N : 2 * N + O]
-        halves = range(N // P)
         p_acc = [psum.tile([P, O], F32, name="p_acc%d" % h) for h in halves]
         for h in halves:
             nc.tensor.matmul_mx(
@@ -190,10 +210,6 @@ def tile_list_gatedmiddle_codednote_further_pagetwice_kernel(
                 start=True,
                 stop=False,
             )
-        page_a = [keep.tile([P, E], F32, name="page_a%d" % h) for h in halves]
-        page_b = [keep.tile([P, E], F32, name="page_b%d" % h) for h in halves]
-        for page in page_a + page_b:
-            nc.vector.memset(page[:], 0.0)
 
         a_term = keep.tile([P, PACK, O], F32)
         gated = keep.tile([P, PACK, O], F32)
@@ -202,21 +218,27 @@ def tile_list_gatedmiddle_codednote_further_pagetwice_kernel(
                 a_term[:, t, :], a_rows[t][:].indirect(idx3[:]), ACT.Copy, scale=sa_col[:, t : t + 1]
             )
             nc.vector.tensor_tensor(gated[:, t, :], a_term[:, t, :], gate[t], ALU.mult)
-        b_term = keep.tile([P, PACK, O], F32)
         for t in range(PACK):
             nc.scalar.activation(
                 b_term[:, t, :], b_rows[t][:].indirect(idx5[:]), ACT.Copy, scale=sb_col[:, t : t + 1]
             )
-        hid_grouped = keep.tile([P, O * PACK], BF16, align_bytes=64)
-        nc.vector.tensor_tensor(
-            hid_grouped[:].rearrange("p (c i t) -> p c t i", i=4, t=PACK),
-            gated[:].rearrange("p t (c i) -> p c t i", i=4),
-            b_term[:].rearrange("p t (c i) -> p c t i", i=4),
-            ALU.min,
-        )
+        hid_grouped = keep.tile([P, O, PACK], BF16, align_bytes=64)
         hid_words = keep.tile([P, O], U32, align_bytes=64)
         hid_scales = keep.tile([P, O], U8, align_bytes=64)
-        nc.vector.quantize_mx(out=hid_words[:].bitcast(FP8X4), scales=hid_scales[:], in_=hid_grouped[:])
+        places = [slice(0, O // 2), slice(O // 2, O)]
+        for cols in places:
+            nc.vector.tensor_tensor(
+                hid_grouped[:, cols, :].rearrange("p (c i) t -> p c t i", i=4),
+                gated[:, :, cols].rearrange("p t (c i) -> p c t i", i=4),
+                b_term[:, :, cols].rearrange("p t (c i) -> p c t i", i=4),
+                ALU.min,
+            )
+        for cols in places:
+            nc.vector.quantize_mx(
+                out=hid_words[:, cols].bitcast(FP8X4),
+                scales=hid_scales[:, cols],
+                in_=hid_grouped[:, cols, :].rearrange("p o t -> p (o t)"),
+            )
 
         p_rows = []
         for h in halves:

from contextlib import ExitStack

import concourse.mybir as mybir

K, T, J, R, F, Z, O, N, L, E = 512, 1024, 256, 512, 512, 1024, 128, 256, 512, 512

FLOPS = 2 * (K * R * J + F * R * J + R * N * O + L * N * O)

F32 = mybir.dt.float32
BF16 = mybir.dt.bfloat16
I32 = mybir.dt.int32
U32 = mybir.dt.uint32
U16 = mybir.dt.uint16
U8 = mybir.dt.uint8
FP8X4 = mybir.dt.float8_e4m3fn_x4
FP4X4 = mybir.dt.float4_e2m1fn_x4
ACT = mybir.ActivationFunctionType
ALU = mybir.AluOpType

P = 128
PACK = 4
QUAD = 32
LIVE = 4


def tile_list_gatedmiddle_codednote_further_pagetwice_kernel(
    tc, xo_words, xo_scales, cq, gs, w_words, w_scales, w2_words, w2_scales, sa, sb, sg, bg,
    wb_words, wb_scales, sx_words, sx_scales, ws_words, ws_scales,
    offs, offs2, offs3, offs4, offs5, offs6, offs7, out,
):
    nc = tc.nc
    with ExitStack() as ctx:
        lists = ctx.enter_context(tc.tile_pool(name="lists", bufs=1))
        keep = ctx.enter_context(tc.tile_pool(name="keep", bufs=1))
        psum = ctx.enter_context(tc.psum_pool(name="psum", bufs=1))

        def load_list(src, name):
            held = lists.tile(list(src.shape), U16, name=name)
            nc.sync.dma_start(held[:], src)
            return held

        def load_words(src, name):
            rows = src[0] if src.ndim == 3 else src[0].rearrange("p n t -> p (n t)")
            held = keep.tile([P, rows.shape[1]], U8, name=name, align_bytes=64)
            nc.sync.dma_start(held[:].bitcast(I32), rows.bitcast(I32))
            return held

        def load_column(src, name, queue):
            held = keep.tile([P, PACK], F32, name=name)
            queue.dma_start(held[:], src.rearrange("(p t) o -> p (t o)", t=PACK))
            return held

        def stage_scales(staged, src, column, queue):
            words = src.shape[2] // 4
            queue.dma_start(
                staged[:, :, column : column + words], src[0].bitcast(I32).rearrange("(q r) n -> r q n", r=LIVE)
            )

        def deal_words(words, name, copy):
            dealt = keep.tile([P, 2 * R], U8, name=name, align_bytes=64)
            copy(
                dealt[:].bitcast(U16).rearrange("p (t m) -> p t m", t=PACK),
                words[:].bitcast(U16).rearrange("p (m t) -> p t m", t=PACK),
            )
            return dealt

        def deal_scales(plane, name):
            dealt = keep.tile([P, R], U8, name=name, align_bytes=64)
            nc.vector.tensor_copy(
                dealt[:].rearrange("p (t m) -> p t m", t=PACK),
                plane.bitcast(U8).rearrange("p (m t) -> p t m", t=PACK),
            )
            return dealt

        def load_cq(t):
            rows = keep.tile([P, T], F32, name="cq%d" % t)
            nc.sync.dma_start(rows[:], cq.rearrange("(p t) c -> p t c", t=PACK)[:, t, :])
            return rows

        xo_scale_rows = xo_scales[0].bitcast(I32).rearrange("(u q r) n -> u r q n", u=2, r=LIVE)
        xo_staged = keep.tile([P, 2, Z // 4], I32)
        nc.scalar.dma_start(xo_staged[0:LIVE], xo_scale_rows[0])
        nc.sync.dma_start(xo_staged[64 : 64 + LIVE], xo_scale_rows[1])
        idx2 = load_list(offs2, "idx2")
        first_staged = keep.tile([LIVE, 4, 2 * R // 4], I32)
        stage_scales(first_staged[:], w2_scales, 0, nc.scalar)
        stage_scales(first_staged[:], w_scales, R // 4, nc.scalar)
        xo_raw = load_words(xo_words, "xo_raw")
        w2_raw = load_words(w2_words, "w2_raw")
        cq_rows = [load_cq(0)]
        idx = load_list(offs, "idx")
        gs_col = load_column(gs, "gs_col", nc.sync)
        cq_rows.extend([load_cq(1), load_cq(2)])
        w_raw = load_words(w_words, "w_raw")
        xo_plane = keep.tile([P, Z], U8)
        nc.vector.memset(xo_plane[:].bitcast(I32), 0)
        first_spread = keep.tile([P, 2 * R // 4], I32)
        nc.vector.memset(first_spread[:], 0)
        last_staged = keep.tile([P, 4, (2 * N + O) // 4], I32, align_bytes=64)
        nc.vector.memset(last_staged[:, 0, :], 0)
        stage_scales(last_staged[0:LIVE], ws_scales, 0, nc.sync)
        cq_rows.append(load_cq(3))
        stage_scales(last_staged[0:LIVE], wb_scales, N // 4, nc.sync)
        stage_scales(last_staged[0:LIVE], sx_scales, 2 * N // 4, nc.sync)
        sg_col = load_column(sg, "sg_col", nc.sync)
        bg_col = load_column(bg, "bg_col", nc.sync)
        idx4 = load_list(offs4, "idx4")
        idx5 = load_list(offs5, "idx5")
        sb_col = load_column(sb, "sb_col", nc.sync)
        idx3 = load_list(offs3, "idx3")
        sa_col = load_column(sa, "sa_col", nc.sync)
        ws_raw = load_words(ws_words, "ws_raw")
        sx_raw = load_words(sx_words, "sx_raw")
        wb_raw = load_words(wb_words, "wb_raw")
        idx6 = load_list(offs6, "idx6")
        idx7 = load_list(offs7, "idx7")

        halves = range(N // P)
        page_a = [keep.tile([P, E], F32, name="page_a%d" % h) for h in halves]
        page_b = [keep.tile([P, E], F32, name="page_b%d" % h) for h in halves]
        for page in page_a + page_b:
            nc.vector.memset(page[:], 0.0)
        warm_in = keep.tile([P, 1], F32)
        warm_out = keep.tile([P, 1], F32)
        nc.vector.memset(warm_in[:], 0.0)
        nc.scalar.activation(warm_out[:], warm_in[:], ACT.Sigmoid)

        for q in range(4):
            first = 64 * (q // 2)
            nc.vector.tensor_copy(
                xo_plane[QUAD * q : QUAD * q + LIVE, :].bitcast(I32), xo_staged[first : first + LIVE, q % 2, :]
            )
        xg_scales = keep.tile([P, J], U8, align_bytes=64)
        nc.vector.tensor_copy(xg_scales[:], xo_plane[:].indirect(idx2[:]))
        xg_words = keep.tile([P, J], U32, align_bytes=64)
        nc.vector.tensor_copy(xg_words[:], xo_raw[:].bitcast(U32).indirect(idx2[:]))
        for q in range(4):
            nc.vector.tensor_copy(first_spread[QUAD * q : QUAD * q + LIVE, :], first_staged[:, q, :])
        w2_plane = deal_scales(first_spread[:, 0 : R // 4], "w2_plane")
        w2_dealt = deal_words(w2_raw, "w2_dealt", nc.scalar.copy)

        def first_stage(words, plane, rhs_words, rhs_scales, name):
            tiles = []
            for t in range(PACK):
                acc = psum.tile([P, J], F32, name="acc%d" % t)
                nc.tensor.matmul_mx(
                    out=acc[:],
                    lhsT=words[:, 2 * P * t : 2 * P * (t + 1)].bitcast(FP4X4),
                    lhsT_scale=plane[:, P * t : P * (t + 1)],
                    rhs=rhs_words[:].bitcast(FP8X4),
                    rhs_scale=rhs_scales[:],
                    start=True,
                    stop=True,
                )
                rows = keep.tile([P, J], F32, name="%s%d" % (name, t))
                nc.vector.tensor_copy(rows[:], acc[:])
                tiles.append(rows)
            return tiles

        b_rows = first_stage(w2_dealt, w2_plane, xg_words, xg_scales, "b")
        w_plane = deal_scales(first_spread[:, R // 4 : 2 * R // 4], "w_plane")

        w_dealt = deal_words(w_raw, "w_dealt", nc.vector.tensor_copy)

        x1_early = keep.tile([P, PACK - 1, J], BF16)
        x1_last = keep.tile([P, J], BF16)
        x1_rows = [x1_early[:, t, :] for t in range(PACK - 1)] + [x1_last[:]]
        for t in range(PACK):
            nc.scalar.activation(x1_rows[t], cq_rows[t][:].indirect(idx[:]), ACT.Copy, scale=gs_col[:, t : t + 1])
        b_term = keep.tile([P, PACK, O], F32)
        gate_tile = keep.tile([P, PACK - 1, O], F32)
        gate = [gate_tile[:, 0, :], gate_tile[:, 1, :], b_term[:, PACK - 1, :], gate_tile[:, 2, :]]
        for t in range(PACK):
            nc.scalar.activation(
                gate[t], b_rows[t][:].indirect(idx4[:]), ACT.Sigmoid,
                bias=bg_col[:, t : t + 1], scale=sg_col[:, t : t + 1],
            )
        x1_grouped = keep.tile([P, J, PACK], BF16, align_bytes=64)
        nc.vector.tensor_copy(
            x1_grouped[:, :, 0 : PACK - 1].rearrange("p (c i) t -> p c t i", i=4),
            x1_early[:].rearrange("p t (c i) -> p c t i", i=4),
        )
        x1_words = keep.tile([P, J], U32, align_bytes=64)
        x1_scales = keep.tile([P, J], U8, align_bytes=64)
        slots = [slice(0, J // 2), slice(J // 2, J)]
        for cols in slots:
            nc.vector.tensor_copy(x1_grouped[:, cols, PACK - 1], x1_last[:, cols])
        for cols in slots:
            nc.vector.quantize_mx(
                out=x1_words[:, cols].bitcast(FP8X4),
                scales=x1_scales[:, cols],
                in_=x1_grouped[:, cols, :].rearrange("p j t -> p (j t)"),
            )
        for q in (1, 2, 3):
            nc.vector.tensor_copy(last_staged[QUAD * q : QUAD * q + LIVE, 0, :], last_staged[0:LIVE, q, :])
        a_rows = first_stage(w_dealt, w_plane, x1_words, x1_scales, "a")

        last_planes = last_staged[:, 0, :].bitcast(U8)
        ws_plane = last_planes[:, 0:N]
        wb_plane = last_planes[:, N : 2 * N]
        sx_plane = last_planes[:, 2 * N : 2 * N + O]
        p_acc = [psum.tile([P, O], F32, name="p_acc%d" % h) for h in halves]
        for h in halves:
            nc.tensor.matmul_mx(
                out=p_acc[h][:],
                lhsT=ws_raw[:, 2 * P * h : 2 * P * (h + 1)].bitcast(FP4X4),
                lhsT_scale=ws_plane[:, P * h : P * (h + 1)],
                rhs=sx_raw[:].bitcast(FP8X4),
                rhs_scale=sx_plane,
                start=True,
                stop=False,
            )

        a_term = keep.tile([P, PACK, O], F32)
        gated = keep.tile([P, PACK, O], F32)
        for t in range(PACK):
            nc.scalar.activation(
                a_term[:, t, :], a_rows[t][:].indirect(idx3[:]), ACT.Copy, scale=sa_col[:, t : t + 1]
            )
            nc.vector.tensor_tensor(gated[:, t, :], a_term[:, t, :], gate[t], ALU.mult)
        for t in range(PACK):
            nc.scalar.activation(
                b_term[:, t, :], b_rows[t][:].indirect(idx5[:]), ACT.Copy, scale=sb_col[:, t : t + 1]
            )
        hid_grouped = keep.tile([P, O, PACK], BF16, align_bytes=64)
        hid_words = keep.tile([P, O], U32, align_bytes=64)
        hid_scales = keep.tile([P, O], U8, align_bytes=64)
        places = [slice(0, O // 2), slice(O // 2, O)]
        for cols in places:
            nc.vector.tensor_tensor(
                hid_grouped[:, cols, :].rearrange("p (c i) t -> p c t i", i=4),
                gated[:, :, cols].rearrange("p t (c i) -> p c t i", i=4),
                b_term[:, :, cols].rearrange("p t (c i) -> p c t i", i=4),
                ALU.min,
            )
        for cols in places:
            nc.vector.quantize_mx(
                out=hid_words[:, cols].bitcast(FP8X4),
                scales=hid_scales[:, cols],
                in_=hid_grouped[:, cols, :].rearrange("p o t -> p (o t)"),
            )

        p_rows = []
        for h in halves:
            nc.tensor.matmul_mx(
                out=p_acc[h][:],
                lhsT=wb_raw[:, 2 * P * h : 2 * P * (h + 1)].bitcast(FP4X4),
                lhsT_scale=wb_plane[:, P * h : P * (h + 1)],
                rhs=hid_words[:].bitcast(FP8X4),
                rhs_scale=hid_scales[:],
                start=False,
                stop=True,
            )
            rows = keep.tile([P, O], F32, name="p_rows%d" % h)
            if h == 0:
                nc.vector.tensor_copy(rows[:], p_acc[h][:])
            else:
                nc.scalar.copy(rows[:], p_acc[h][:])
            p_rows.append(rows)
        for h in halves:
            nc.scalar.activation(page_a[h][:].indirect(idx6[:]), p_rows[h][:], ACT.Copy)
            nc.vector.tensor_copy(page_b[h][:].indirect(idx7[:]), p_rows[h][:])
        for h in halves:
            for c in range(2):
                cols = slice(c * E // 2, (c + 1) * E // 2)
                total = keep.tile([P, E // 2], F32, name="total%d%d" % (h, c))
                nc.vector.tensor_tensor(total[:], page_a[h][:, cols], page_b[h][:, cols], ALU.add)
                queue = nc.sync if c == 0 else nc.scalar
                queue.dma_start(out[P * h : P * (h + 1), cols], total[:])
